import numpy as np
import ml_dtypes


def mxq(x, axis, fmt="e4m3"):
    dtype, down = {"e4m3": (ml_dtypes.float8_e4m3fn, 7), "e5m2": (ml_dtypes.float8_e5m2, 14)}[fmt]
    v = np.moveaxis(np.asarray(x, np.float32).astype(ml_dtypes.bfloat16).astype(np.float64), axis, -1)
    blocks = v.reshape(v.shape[:-1] + (-1, 32))
    amax = np.abs(blocks).max(-1, keepdims=True)
    byte = np.maximum(np.where(amax > 0, np.frexp(amax)[1] - 1 + 127, 0) - down, 1)
    scale = np.exp2(byte - 127.0)
    codes = (blocks / scale).astype(np.float32).astype(dtype).astype(np.float64)
    return np.moveaxis((codes * scale).reshape(v.shape), -1, axis)


WIDE = False


def mx_kscale(k):
    if not WIDE:
        return np.ones(k)
    levels = np.array([10, -10, 5, -5, 0])
    if k % 512:
        return np.exp2(np.random.permutation(np.resize(levels, k // 32))).repeat(32)
    a = np.empty((k // 512, 16))
    for p in range(k // 512):
        a[p, :8] = np.random.permutation(np.resize(levels, 8))
        for g in range(8):
            far = levels[np.abs(levels - a[p, g]) >= 10]
            a[p, g + 8] = far[np.random.randint(len(far))]
    return np.exp2(a.ravel()).repeat(32)


BF16 = ml_dtypes.bfloat16


def bf(x):
    return np.asarray(x, np.float32).astype(BF16)


def f64(x):
    return np.asarray(x).astype(np.float64)

def planes(Y):
    n, m = Y.shape
    b = f64(bf(Y)).reshape(n // 32, 32, m)
    amax = np.abs(b).max(1)
    byte = np.clip(np.where(amax > 0, np.frexp(amax)[1] - 1 + 127 - 7, 1), 1, 254)
    codes = (b * np.exp2(127.0 - byte)[:, None, :]).reshape(n, m).astype(np.float32).astype(ml_dtypes.float8_e4m3fn).view(np.uint8)
    words = codes.reshape(n // 512, 128, 4, m).transpose(0, 1, 3, 2)
    return np.ascontiguousarray(words), np.ascontiguousarray(byte.astype(np.uint8).reshape(n // 512, 16, m))


T, K, C = 3072, 2048, 512

LOW, HIGH = -1.0, 1.0


def setup_inputs():
    s = mx_kscale(K)
    link = np.random.randn(T, K) ** 2 / np.sqrt(3.0 * K)
    label = 0.7 * np.random.randn(K, C)
    offset = 0.3 * np.random.randn(C)
    weight = np.exp(0.8 * np.random.randn(T))
    return {
        "two_hop": bf(link * s[None, :]),
        "labels": bf(label / s[:, None]),
        "class_offset": bf(offset),
        "node_weight": bf(weight),
    }


def reference(two_hop, labels, class_offset, node_weight):
    a = mxq(f64(two_hop), axis=1, fmt="e4m3")
    b = mxq(f64(labels), axis=0, fmt="e4m3")
    z = (a @ b) + f64(class_offset)[None, :]
    p = np.minimum(np.maximum(z, LOW), HIGH)
    y = p * f64(node_weight)[:, None]
    Y = y
    words, scales = planes(Y)
    return y, words, scales

@@ -1,0 +1,290 @@
+from contextlib import ExitStack
+
+import concourse.mybir as mybir
+from concourse.masks import make_identity
+
+T, K, C = 3072, 2048, 512
+FLOPS = 2 * T * K * C
+
+F32 = mybir.dt.float32
+BF16 = mybir.dt.bfloat16
+U32 = mybir.dt.uint32
+I32 = mybir.dt.int32
+U8 = mybir.dt.uint8
+FP8X4 = mybir.dt.float8_e4m3fn_x4
+ALU = mybir.AluOpType
+ACT = mybir.ActivationFunctionType
+
+P = 128
+PACK = 4
+K_PASS = P * PACK
+PASSES = K // K_PASS
+GROUPS = T // K_PASS
+PAIRS = 2 * GROUPS
+K_HALF = K // 2
+HALF = C // 2
+B_VECTOR_COLS = 320
+HEAD_PAIRS = 3
+
+
+def tile_clamped_two_hop_labels_g2_kernel(tc, two_hop, labels, class_offset, node_weight,
+                                                     out_0, out_1, out_2):
+    nc = tc.nc
+    a_rows = two_hop.rearrange("(g p t) k -> g p t k", p=P, t=PACK)
+    y_rows = out_0.rearrange("(g p t) c -> g p t c", p=P, t=PACK)
+
+    with ExitStack() as ctx:
+        keep = ctx.enter_context(tc.tile_pool(name="keep", bufs=1))
+        work = ctx.enter_context(tc.tile_pool(name="work", bufs=2))
+        psum = ctx.enter_context(tc.psum_pool(name="psum", bufs=4))
+        ctx.enter_context(tc.manual_schedule())
+
+        ident = keep.tile([P, P], F32, name="ident")
+        make_identity(nc, ident[:])
+
+        offset_raw = keep.tile([P, PACK], BF16, name="offset_raw")
+        nc.scalar.dma_start(out=offset_raw[:], in_=class_offset.rearrange("(p j) -> p j", j=PACK))
+        weight_raw = keep.tile([P, GROUPS, 16], BF16, name="weight_raw")
+        nc.scalar.dma_start(out=weight_raw[:, :, 0:PACK],
+                            in_=node_weight.rearrange("(g p t) -> p g t", p=P, t=PACK))
+
+        a_words = {}
+        b_raw = {}
+
+        def load_half(pair, kh):
+            g, t0 = pair // 2, 2 * (pair % 2)
+            raw = keep.tile([P, 2, K_HALF], BF16, name="a_half_%d_%d" % (pair, kh))
+            nc.sync.dma_start(out=raw[:], in_=a_rows[g, :, t0:t0 + 2, kh * K_HALF:(kh + 1) * K_HALF])
+            a_words[pair, kh] = raw[:].bitcast(F32)
+
+        def load_pair(pair):
+            g, t0 = pair // 2, 2 * (pair % 2)
+            raw = keep.tile([P, 2, K], BF16, name="a_pair_%d" % pair)
+            nc.sync.dma_start(out=raw[:], in_=a_rows[g, :, t0:t0 + 2, :])
+            words = raw[:].bitcast(F32)
+            for kh in range(2):
+                a_words[pair, kh] = words[:, :, kh * K_HALF // 2:(kh + 1) * K_HALF // 2]
+
+        def load_labels(c):
+            raw = keep.tile([P, PACK, C], BF16, name="b_raw_%d" % c)
+            nc.sync.dma_start(out=raw[:], in_=labels[c * K_PASS:(c + 1) * K_PASS, :].rearrange("(p j) n -> p j n", j=PACK))
+            b_raw[c] = raw
+
+        for c in range(PASSES):
+            load_half(c % 2, c // 2)
+            load_labels(c)
+        load_half(2, 0)
+        load_half(2, 1)
+        for pair in range(HEAD_PAIRS, PAIRS):
+            load_pair(pair)
+
+        offset_col = keep.tile([P, PACK], F32, name="offset_col")
+        nc.vector.tensor_copy(out=offset_col[:], in_=offset_raw[:])
+        spread = psum.tile([P, PACK, P], F32, tag="turn", name="spread")
+        for j in range(PACK):
+            nc.tensor.transpose(spread[:, j, :], offset_col[:, j:j + 1].to_broadcast([P, P]), ident[:])
+        weight = keep.tile([P, GROUPS, PACK], F32, name="weight")
+        nc.vector.tensor_copy(out=weight[:], in_=weight_raw[:, :, 0:PACK])
+        offset = keep.tile([P, C], F32, name="offset")
+        nc.vector.tensor_copy(out=offset[:].rearrange("m (p j) -> m p j", j=PACK),
+                              in_=spread[:].rearrange("m j p -> m p j"))
+        upper = keep.tile([P, GROUPS, PACK], F32, name="upper")
+        lower = keep.tile([P, GROUPS, PACK], F32, name="lower")
+        nc.vector.scalar_tensor_tensor(out=upper[:], in0=weight[:], scalar=-1.0, in1=weight[:], op0=ALU.mult, op1=ALU.max)
+        nc.vector.scalar_tensor_tensor(out=lower[:], in0=weight[:], scalar=-1.0, in1=weight[:], op0=ALU.mult, op1=ALU.min)
+
+        a_grouped, a_codes, a_scales = {}, {}, {}
+        b_grouped, b_codes, b_scales = {}, {}, {}
+        acc, shift, y, y_grouped, y_codes = {}, {}, {}, {}, {}
+        y_scales = keep.tile([P, GROUPS - 1, C], U8, name="y_scales", align_bytes=64)
+        y_scales_last = keep.tile([P, C], U8, name="y_scales_last", align_bytes=64)
+
+        def turn(pair, kh):
+            words = a_words[pair, kh]
+            grouped = work.tile([P, 2, 2 * P * PACK], BF16, tag="a_grouped", name="a_grouped", bufs=3, align_bytes=64)
+            for tl in range(2):
+                bank = psum.tile([P, 2, 2, P], F32, tag="turn", name="bank")
+                for cl in range(2):
+                    for u in range(2):
+                        nc.tensor.transpose(bank[:, cl, u, :], words[:, tl, 256 * cl + u:256 * (cl + 1):2], ident[:])
+                nc.scalar.copy(out=grouped[:, tl, :].bitcast(F32).rearrange("p (c r u) -> p c r u", c=2, u=2),
+                               in_=bank[:].rearrange("p c u r -> p c r u"))
+            a_grouped[pair, kh] = grouped
+
+        def quantize_a(pair, kh):
+            codes = work.tile([P, 4 * P], U32, tag="a_codes", name="a_codes", bufs=6, align_bytes=64)
+            scales = work.tile([P, 4 * P], U8, tag="a_scales", name="a_scales", bufs=6, align_bytes=64)
+            nc.vector.quantize_mx(out=codes[:].bitcast(FP8X4), scales=scales[:],
+                                  in_=a_grouped[pair, kh][:].rearrange("p t x -> p (t x)"))
+            a_codes[pair, kh], a_scales[pair, kh] = codes, scales
+
+        def interleave(copy, dst, src, lo, hi):
+            copy(out=dst[:, lo:hi, :].rearrange("p (c i) t -> p c t i", i=4),
+                 in_=src[:, :, lo:hi].rearrange("p t (c i) -> p c t i", i=4))
+
+        def group_b_vector(c):
+            grouped = work.tile([P, C, PACK], BF16, tag="b_grouped", name="b_grouped", bufs=2, align_bytes=64)
+            interleave(nc.vector.tensor_copy, grouped, b_raw[c], 0, B_VECTOR_COLS)
+            b_grouped[c] = grouped
+
+        def group_b_scalar(c):
+            interleave(nc.scalar.copy, b_grouped[c], b_raw[c], B_VECTOR_COLS, C)
+
+        def quantize_b(c):
+            codes = keep.tile([P, C], U32, name="b_codes_%d" % c, align_bytes=64)
+            scales = keep.tile([P, C], U8, name="b_scales_%d" % c, align_bytes=64)
+            nc.vector.quantize_mx(out=codes[:].bitcast(FP8X4), scales=scales[:],
+                                  in_=b_grouped[c][:].rearrange("p n j -> p (n j)"))
+            b_codes[c], b_scales[c] = codes, scales
+
+        def multiply(i, c, lo=0, hi=C, tag="acc"):
+            if c == 0:
+                bank = psum.tile([P, hi - lo], F32, tag=tag, name="acc_bank")
+                acc[i, lo] = bank
+            slot = 2 * (i % 2) + c % 2
+            cols = slice(slot * P, (slot + 1) * P)
+            nc.tensor.matmul_mx(out=acc[i, lo][:],
+                                lhsT=a_codes[i // 2, c // 2][:, cols].bitcast(FP8X4),
+                                lhsT_scale=a_scales[i // 2, c // 2][:, cols],
+                                rhs=b_codes[c][:, lo:hi].bitcast(FP8X4), rhs_scale=b_scales[c][:, lo:hi],
+                                start=(c == 0), stop=(c == PASSES - 1))
+
+        def make_shift(i):
+            tile_shift = work.tile([P, C], F32, tag="shift", name="tile_shift", bufs=6)
+            nc.scalar.activation(out=tile_shift[:], in_=offset[:], func=ACT.Copy, scale=weight[:, i // 4, i % 4:i % 4 + 1])
+            shift[i] = tile_shift
+
+        def leave_psum(i, lo=0, hi=C):
+            g, t = i // 4, i % 4
+            if g not in y:
+                y_group = work.tile([P, PACK, C], F32, tag="y", name="y_group", bufs=4)
+                y[g] = y_group
+            nc.vector.scalar_tensor_tensor(out=y[g][:, t, lo:hi], in0=acc[i, lo][:], scalar=weight[:, g, t:t + 1],
+                                           in1=shift[i][:, lo:hi], op0=ALU.mult, op1=ALU.add)
+
+        def clamp(i, lo=0, hi=C):
+            g, t = i // 4, i % 4
+            nc.vector.tensor_scalar(out=y[g][:, t, lo:hi], in0=y[g][:, t, lo:hi], scalar1=lower[:, g, t:t + 1],
+                                    scalar2=upper[:, g, t:t + 1], op0=ALU.max, op1=ALU.min)
+
+        def group_y(copy, g, lo, hi):
+            if g not in y_grouped:
+                grouped = work.tile([P, C, PACK], BF16, tag="y_grouped", name="y_grouped_tile", bufs=2, align_bytes=64)
+                y_grouped[g] = grouped
+            interleave(copy, y_grouped[g], y[g], lo, hi)
+
+        def quantize_y(g, lo=0, hi=C):
+            if g not in y_codes:
+                codes = keep.tile([P, C], U32, name="y_codes_%d" % g, align_bytes=64)
+                y_codes[g] = codes
+            scales = y_scales_last[:, lo:hi] if g == GROUPS - 1 else y_scales[:, g, lo:hi]
+            nc.vector.quantize_mx(out=y_codes[g][:, lo:hi].bitcast(FP8X4), scales=scales,
+                                  in_=y_grouped[g][:, lo:hi, :].rearrange("p n j -> p (n j)"))
+
+        def store_y(g, t0=0, t1=PACK, lo=0, hi=C):
+            nc.sync.dma_start(out=y_rows[g, :, t0:t1, lo:hi], in_=y[g][:, t0:t1, lo:hi])
+
+        def store_words(g, lo=0, hi=C):
+            nc.sync.dma_start(out=out_1[g, :, lo:hi, :].rearrange("p m t -> p (m t)").bitcast(I32),
+                              in_=y_codes[g][:, lo:hi].bitcast(I32))
+
+        for c in range(PASSES):
+            turn(c % 2, c // 2)
+            group_b_vector(c)
+            group_b_scalar(c)
+            quantize_a(c % 2, c // 2)
+            quantize_b(c)
+            if c == 1:
+                multiply(0, 0)
+                multiply(1, 0)
+            if c == 2:
+                multiply(2, 0)
+                multiply(3, 0)
+                for i in range(4):
+                    multiply(i, 1)
+            if c == 3:
+                multiply(0, 2)
+                multiply(1, 2)
+        turn(2, 0)
+        make_shift(0)
+        quantize_a(2, 0)
+        turn(2, 1)
+        make_shift(1)
+        multiply(0, 3)
+        multiply(1, 3)
+        for i in (2, 3):
+            multiply(i, 2)
+            multiply(i, 3)
+        quantize_a(2, 1)
+        leave_psum(0)
+        leave_psum(1)
+        make_shift(2)
+        make_shift(3)
+        clamp(0)
+        clamp(1)
+
+        last = PAIRS - 1
+        for pair in range(2, last):
+            done = pair - 1
+            g = done // 2
+            leave_psum(2 * done)
+            if done % 2 == 0:
+                quantize_y(g - 1)
+                store_words(g - 1)
+            leave_psum(2 * done + 1)
+            clamp(2 * done)
+            clamp(2 * done + 1)
+            if done % 2 == 1:
+                store_y(g)
+                group_y(nc.vector.tensor_copy, g, 0, HALF)
+            if pair == 2:
+                make_shift(4)
+                make_shift(5)
+            turn(pair + 1, 0)
+            quantize_a(pair + 1, 0)
+            turn(pair + 1, 1)
+            quantize_a(pair + 1, 1)
+            if done % 2 == 1:
+                group_y(nc.scalar.copy, g, HALF, C)
+            make_shift(2 * pair + 2)
+            make_shift(2 * pair + 3)
+            for i in (2 * pair, 2 * pair + 1):
+                for c in range(PASSES):
+                    multiply(i, c)
+
+        g = GROUPS - 1
+        first, second = 2 * last, 2 * last + 1
+        for lo, tag in ((0, "acc"), (HALF, "turn")):
+            for i in (first, second):
+                for c in range(PASSES):
+                    multiply(i, c, lo, lo + HALF, tag)
+        leave_psum(first - 2)
+        quantize_y(g - 1)
+        store_words(g - 1)
+        for q in range(4):
+            nc.sync.dma_start(out=out_2[0:g, 4 * q:4 * q + 4, :].rearrange("g r m -> r g m").bitcast(I32),
+                              in_=y_scales[32 * q:32 * q + 4, :, :].bitcast(I32))
+        leave_psum(first - 1)
+        clamp(first - 2)
+        leave_psum(first, 0, HALF)
+        clamp(first - 1)
+        store_y(g, 0, 2)
+        leave_psum(second, 0, HALF)
+        clamp(first, 0, HALF)
+        clamp(second, 0, HALF)
+        store_y(g, 2, 4, 0, HALF)
+        group_y(nc.scalar.copy, g, 0, HALF)
+        leave_psum(first, HALF, C)
+        leave_psum(second, HALF, C)
+        clamp(first, HALF, C)
+        clamp(second, HALF, C)
+        store_y(g, 2, 4, HALF, C)
+        group_y(nc.vector.tensor_copy, g, HALF, C)
+        quantize_y(g, 0, HALF)
+        store_words(g, 0, HALF)
+        quantize_y(g, HALF, C)
+        store_words(g, HALF, C)
+        for q in range(4):
+            queue = nc.scalar if q < 2 else nc.sync
+            queue.dma_start(out=out_2[g, 4 * q:4 * q + 4, :].bitcast(I32),
+                            in_=y_scales_last[32 * q:32 * q + 4, :].bitcast(I32))

@@ -20,11 +20,16 @@ PACK = 4
 K_PASS = P * PACK
 PASSES = K // K_PASS
 GROUPS = T // K_PASS
-PAIRS = 2 * GROUPS
+TILES = T // P
 K_HALF = K // 2
 HALF = C // 2
+LAST_GROUP = GROUPS - 1
+LAST = TILES - 1
 B_VECTOR_COLS = 320
-HEAD_PAIRS = 3
+SINGLE_TILES = 6
+PAIR_BUFS = 6
+COMPACT_FROM, COMPACT_TO = 10, 22
+SHIFT_AHEAD = 6
 
 
 def tile_clamped_two_hop_labels_g2_kernel(tc, two_hop, labels, class_offset, node_weight,
@@ -48,87 +53,101 @@ def tile_clamped_two_hop_labels_g2_kernel(tc, two_hop, labels, class_offset, nod
         nc.scalar.dma_start(out=weight_raw[:, :, 0:PACK],
                             in_=node_weight.rearrange("(g p t) -> p g t", p=P, t=PACK))
 
-        a_words = {}
-        b_raw = {}
+        a_words, a_odd, a_grouped, a_codes, a_scales = {}, {}, {}, {}, {}
+        b_raw, b_grouped, b_codes, b_scales = {}, {}, {}, {}
+        acc, shift, y, y_grouped, y_codes = {}, {}, {}, {}, {}
 
-        def load_half(pair, kh):
-            g, t0 = pair // 2, 2 * (pair % 2)
-            raw = keep.tile([P, 2, K_HALF], BF16, name="a_half_%d_%d" % (pair, kh))
-            nc.sync.dma_start(out=raw[:], in_=a_rows[g, :, t0:t0 + 2, kh * K_HALF:(kh + 1) * K_HALF])
-            a_words[pair, kh] = raw[:].bitcast(F32)
+        def load_half(i, kh):
+            raw = keep.tile([P, K_HALF], BF16, name="a_half_%d_%d" % (i, kh))
+            nc.sync.dma_start(out=raw[:], in_=a_rows[0, :, i, kh * K_HALF:(kh + 1) * K_HALF])
+            a_words[i, kh] = raw[:].bitcast(F32)
 
-        def load_pair(pair):
-            g, t0 = pair // 2, 2 * (pair % 2)
-            raw = keep.tile([P, 2, K], BF16, name="a_pair_%d" % pair)
-            nc.sync.dma_start(out=raw[:], in_=a_rows[g, :, t0:t0 + 2, :])
-            words = raw[:].bitcast(F32)
-            for kh in range(2):
-                a_words[pair, kh] = words[:, :, kh * K_HALF // 2:(kh + 1) * K_HALF // 2]
+        def load_tiles(first, count):
+            g, t = first // PACK, first % PACK
+            raw = work.tile([P, count, K], BF16, tag="a_raw_%d" % count, name="raw", bufs=PAIR_BUFS if count == 2 else 2)
+            nc.sync.dma_start(out=raw[:], in_=a_rows[g, :, t:t + count, :])
+            for n in range(count):
+                a_words[first + n] = raw[:, n, :].bitcast(F32)
+                for kh in range(2):
+                    a_words[first + n, kh] = a_words[first + n][:, kh * K_HALF // 2:(kh + 1) * K_HALF // 2]
 
         def load_labels(c):
             raw = keep.tile([P, PACK, C], BF16, name="b_raw_%d" % c)
-            nc.sync.dma_start(out=raw[:], in_=labels[c * K_PASS:(c + 1) * K_PASS, :].rearrange("(p j) n -> p j n", j=PACK))
+            nc.sync.dma_start(out=raw[:],
+                              in_=labels[c * K_PASS:(c + 1) * K_PASS, :].rearrange("(p j) n -> p j n", j=PACK))
             b_raw[c] = raw
 
-        for c in range(PASSES):
-            load_half(c % 2, c // 2)
+        load_labels(0)
+        for i in range(PACK):
+            load_half(i, 0)
+        load_labels(1)
+        for c in (2, 3):
+            load_half(2 * c - 4, 1)
+            load_half(2 * c - 3, 1)
             load_labels(c)
-        load_half(2, 0)
-        load_half(2, 1)
-        for pair in range(HEAD_PAIRS, PAIRS):
-            load_pair(pair)
+        for i in range(PACK, SINGLE_TILES):
+            load_tiles(i, 1)
+        for i in range(SINGLE_TILES, SINGLE_TILES + 2 * PAIR_BUFS, 2):
+            load_tiles(i, 2)
 
         offset_col = keep.tile([P, PACK], F32, name="offset_col")
         nc.vector.tensor_copy(out=offset_col[:], in_=offset_raw[:])
         spread = psum.tile([P, PACK, P], F32, tag="turn", name="spread")
         for j in range(PACK):
             nc.tensor.transpose(spread[:, j, :], offset_col[:, j:j + 1].to_broadcast([P, P]), ident[:])
-        weight = keep.tile([P, GROUPS, PACK], F32, name="weight")
-        nc.vector.tensor_copy(out=weight[:], in_=weight_raw[:, :, 0:PACK])
         offset = keep.tile([P, C], F32, name="offset")
-        nc.vector.tensor_copy(out=offset[:].rearrange("m (p j) -> m p j", j=PACK),
-                              in_=spread[:].rearrange("m j p -> m p j"))
+        weight = keep.tile([P, GROUPS, PACK], F32, name="weight")
         upper = keep.tile([P, GROUPS, PACK], F32, name="upper")
         lower = keep.tile([P, GROUPS, PACK], F32, name="lower")
+        nc.vector.tensor_copy(out=weight[:], in_=weight_raw[:, :, 0:PACK])
         nc.vector.scalar_tensor_tensor(out=upper[:], in0=weight[:], scalar=-1.0, in1=weight[:], op0=ALU.mult, op1=ALU.max)
         nc.vector.scalar_tensor_tensor(out=lower[:], in0=weight[:], scalar=-1.0, in1=weight[:], op0=ALU.mult, op1=ALU.min)
 
-        a_grouped, a_codes, a_scales = {}, {}, {}
-        b_grouped, b_codes, b_scales = {}, {}, {}
-        acc, shift, y, y_grouped, y_codes = {}, {}, {}, {}, {}
-        y_scales = keep.tile([P, GROUPS - 1, C], U8, name="y_scales", align_bytes=64)
-        y_scales_last = keep.tile([P, C], U8, name="y_scales_last", align_bytes=64)
+        y_scales_early = keep.tile([P, GROUPS - 2, C], U8, name="y_scales_early", align_bytes=64)
+        y_scales_late = keep.tile([P, 2, C], U8, name="y_scales_late", align_bytes=64)
 
-        def turn(pair, kh):
-            words = a_words[pair, kh]
-            grouped = work.tile([P, 2, 2 * P * PACK], BF16, tag="a_grouped", name="a_grouped", bufs=3, align_bytes=64)
-            for tl in range(2):
-                bank = psum.tile([P, 2, 2, P], F32, tag="turn", name="bank")
-                for cl in range(2):
-                    for u in range(2):
-                        nc.tensor.transpose(bank[:, cl, u, :], words[:, tl, 256 * cl + u:256 * (cl + 1):2], ident[:])
-                nc.scalar.copy(out=grouped[:, tl, :].bitcast(F32).rearrange("p (c r u) -> p c r u", c=2, u=2),
-                               in_=bank[:].rearrange("p c u r -> p c r u"))
-            a_grouped[pair, kh] = grouped
+        def compact(i):
+            if COMPACT_FROM <= i < COMPACT_TO:
+                odd = work.tile([P, PASSES * P], F32, tag="a_odd", name="odd", bufs=4)
+                nc.vector.tensor_copy(out=odd[:], in_=a_words[i][:, 1::2])
+                a_odd[i] = odd
 
-        def quantize_a(pair, kh):
-            codes = work.tile([P, 4 * P], U32, tag="a_codes", name="a_codes", bufs=6, align_bytes=64)
-            scales = work.tile([P, 4 * P], U8, tag="a_scales", name="a_scales", bufs=6, align_bytes=64)
-            nc.vector.quantize_mx(out=codes[:].bitcast(FP8X4), scales=scales[:],
-                                  in_=a_grouped[pair, kh][:].rearrange("p t x -> p (t x)"))
-            a_codes[pair, kh], a_scales[pair, kh] = codes, scales
+        def turn_half(i, kh, grouped):
+            bank = psum.tile([P, 2, 2, P], F32, tag="turn", name="bank")
+            for cl in range(2):
+                words = a_words[i, kh][:, 2 * P * cl:2 * P * (cl + 1)]
+                c = 2 * kh + cl
+                nc.tensor.transpose(bank[:, cl, 0, :], words[:, 0::2], ident[:])
+                nc.tensor.transpose(bank[:, cl, 1, :],
+                                    a_odd[i][:, c * P:(c + 1) * P] if i in a_odd else words[:, 1::2], ident[:])
+            nc.scalar.copy(out=grouped.bitcast(F32).rearrange("p (c r u) -> p c r u", c=2, u=2),
+                           in_=bank[:].rearrange("p c u r -> p c r u"))
 
-        def interleave(copy, dst, src, lo, hi):
-            copy(out=dst[:, lo:hi, :].rearrange("p (c i) t -> p c t i", i=4),
-                 in_=src[:, :, lo:hi].rearrange("p t (c i) -> p c t i", i=4))
+        def turn(i, halves=(0, 1)):
+            grouped = work.tile([P, len(halves) * K_HALF], BF16, tag="a_grouped", name="grouped", bufs=4, align_bytes=64)
+            for n, kh in enumerate(halves):
+                turn_half(i, kh, grouped[:, n * K_HALF:(n + 1) * K_HALF])
+            a_grouped[i] = grouped
+
+        def quantize_a(i, halves=(0, 1)):
+            if halves[0] == 0:
+                codes = work.tile([P, PASSES * P], U32, tag="a_codes", name="codes", bufs=6, align_bytes=64)
+                scales = work.tile([P, PASSES * P], U8, tag="a_scales", name="scales", bufs=6, align_bytes=64)
+                a_codes[i], a_scales[i] = codes, scales
+            cols = slice(2 * P * halves[0], 2 * P * (halves[-1] + 1))
+            nc.vector.quantize_mx(out=a_codes[i][:, cols].bitcast(FP8X4), scales=a_scales[i][:, cols],
+                                  in_=a_grouped[i][:])
+
+        def interleave(copy, dst, src):
+            copy(out=dst.rearrange("p (c i) t -> p c t i", i=4), in_=src.rearrange("p t (c i) -> p c t i", i=4))
 
         def group_b_vector(c):
-            grouped = work.tile([P, C, PACK], BF16, tag="b_grouped", name="b_grouped", bufs=2, align_bytes=64)
-            interleave(nc.vector.tensor_copy, grouped, b_raw[c], 0, B_VECTOR_COLS)
+            grouped = work.tile([P, C, PACK], BF16, tag="b_grouped", name="b_grouped_tile", align_bytes=64)
+            interleave(nc.vector.tensor_copy, grouped[:, :B_VECTOR_COLS, :], b_raw[c][:, :, :B_VECTOR_COLS])
             b_grouped[c] = grouped
 
         def group_b_scalar(c):
-            interleave(nc.scalar.copy, b_grouped[c], b_raw[c], B_VECTOR_COLS, C)
+            interleave(nc.scalar.copy, b_grouped[c][:, B_VECTOR_COLS:, :], b_raw[c][:, :, B_VECTOR_COLS:])
 
         def quantize_b(c):
             codes = keep.tile([P, C], U32, name="b_codes_%d" % c, align_bytes=64)
@@ -141,150 +160,169 @@ def tile_clamped_two_hop_labels_g2_kernel(tc, two_hop, labels, class_offset, nod
             if c == 0:
                 bank = psum.tile([P, hi - lo], F32, tag=tag, name="acc_bank")
                 acc[i, lo] = bank
-            slot = 2 * (i % 2) + c % 2
-            cols = slice(slot * P, (slot + 1) * P)
+            cols = slice(c * P, (c + 1) * P)
             nc.tensor.matmul_mx(out=acc[i, lo][:],
-                                lhsT=a_codes[i // 2, c // 2][:, cols].bitcast(FP8X4),
-                                lhsT_scale=a_scales[i // 2, c // 2][:, cols],
+                                lhsT=a_codes[i][:, cols].bitcast(FP8X4), lhsT_scale=a_scales[i][:, cols],
                                 rhs=b_codes[c][:, lo:hi].bitcast(FP8X4), rhs_scale=b_scales[c][:, lo:hi],
                                 start=(c == 0), stop=(c == PASSES - 1))
 
-        def make_shift(i):
-            tile_shift = work.tile([P, C], F32, tag="shift", name="tile_shift", bufs=6)
-            nc.scalar.activation(out=tile_shift[:], in_=offset[:], func=ACT.Copy, scale=weight[:, i // 4, i % 4:i % 4 + 1])
-            shift[i] = tile_shift
+        def all_passes(i, lo=0, hi=C, tag="acc"):
+            for c in range(PASSES):
+                multiply(i, c, lo, hi, tag)
+
+        def make_shifts(upto, most):
+            for i in range(len(shift), min(len(shift) + most, upto, TILES)):
+                tile_shift = work.tile([P, C], F32, tag="shift", name="tile_shift", bufs=8)
+                nc.scalar.activation(out=tile_shift[:], in_=offset[:], func=ACT.Copy,
+                                     scale=weight[:, i // PACK, i % PACK:i % PACK + 1])
+                shift[i] = tile_shift
+
+        def y_part(i, lo, hi):
+            g, t = i // PACK, i % PACK
+            if g == LAST_GROUP:
+                return y[g][:, lo // HALF:hi // HALF, t, :]
+            return y[g][:, t, lo:hi].rearrange("p (h c) -> p h c", c=HALF)
+
+        def y_half(g, h):
+            return y[g][:, h, :, :] if g == LAST_GROUP else y[g][:, :, h * HALF:(h + 1) * HALF]
 
         def leave_psum(i, lo=0, hi=C):
-            g, t = i // 4, i % 4
+            g, t = i // PACK, i % PACK
             if g not in y:
-                y_group = work.tile([P, PACK, C], F32, tag="y", name="y_group", bufs=4)
+                y_group = work.tile([P, 2, PACK, HALF] if g == LAST_GROUP else [P, PACK, C], F32, tag="y",
+                                    name="y_group", bufs=4)
                 y[g] = y_group
-            nc.vector.scalar_tensor_tensor(out=y[g][:, t, lo:hi], in0=acc[i, lo][:], scalar=weight[:, g, t:t + 1],
-                                           in1=shift[i][:, lo:hi], op0=ALU.mult, op1=ALU.add)
+            nc.vector.scalar_tensor_tensor(out=y_part(i, lo, hi), in0=acc[i, lo][:].rearrange("p (h c) -> p h c", c=HALF),
+                                           scalar=weight[:, g, t:t + 1],
+                                           in1=shift[i][:, lo:hi].rearrange("p (h c) -> p h c", c=HALF),
+                                           op0=ALU.mult, op1=ALU.add)
 
         def clamp(i, lo=0, hi=C):
-            g, t = i // 4, i % 4
-            nc.vector.tensor_scalar(out=y[g][:, t, lo:hi], in0=y[g][:, t, lo:hi], scalar1=lower[:, g, t:t + 1],
+            g, t = i // PACK, i % PACK
+            nc.vector.tensor_scalar(out=y_part(i, lo, hi), in0=y_part(i, lo, hi), scalar1=lower[:, g, t:t + 1],
                                     scalar2=upper[:, g, t:t + 1], op0=ALU.max, op1=ALU.min)
 
-        def group_y(copy, g, lo, hi):
+        def group_y(copy, g, h):
             if g not in y_grouped:
-                grouped = work.tile([P, C, PACK], BF16, tag="y_grouped", name="y_grouped_tile", bufs=2, align_bytes=64)
+                grouped = work.tile([P, C, PACK], BF16, tag="y_grouped", name="y_grouped_tile", align_bytes=64)
                 y_grouped[g] = grouped
-            interleave(copy, y_grouped[g], y[g], lo, hi)
+            interleave(copy, y_grouped[g][:, h * HALF:(h + 1) * HALF, :], y_half(g, h))
 
         def quantize_y(g, lo=0, hi=C):
             if g not in y_codes:
                 codes = keep.tile([P, C], U32, name="y_codes_%d" % g, align_bytes=64)
                 y_codes[g] = codes
-            scales = y_scales_last[:, lo:hi] if g == GROUPS - 1 else y_scales[:, g, lo:hi]
+            scales = y_scales_early[:, g, lo:hi] if g < GROUPS - 2 else y_scales_late[:, g - (GROUPS - 2), lo:hi]
             nc.vector.quantize_mx(out=y_codes[g][:, lo:hi].bitcast(FP8X4), scales=scales,
                                   in_=y_grouped[g][:, lo:hi, :].rearrange("p n j -> p (n j)"))
-
-        def store_y(g, t0=0, t1=PACK, lo=0, hi=C):
-            nc.sync.dma_start(out=y_rows[g, :, t0:t1, lo:hi], in_=y[g][:, t0:t1, lo:hi])
-
-        def store_words(g, lo=0, hi=C):
             nc.sync.dma_start(out=out_1[g, :, lo:hi, :].rearrange("p m t -> p (m t)").bitcast(I32),
                               in_=y_codes[g][:, lo:hi].bitcast(I32))
 
-        for c in range(PASSES):
-            turn(c % 2, c // 2)
-            group_b_vector(c)
-            group_b_scalar(c)
-            quantize_a(c % 2, c // 2)
-            quantize_b(c)
-            if c == 1:
-                multiply(0, 0)
-                multiply(1, 0)
-            if c == 2:
-                multiply(2, 0)
-                multiply(3, 0)
-                for i in range(4):
-                    multiply(i, 1)
-            if c == 3:
-                multiply(0, 2)
-                multiply(1, 2)
-        turn(2, 0)
-        make_shift(0)
-        quantize_a(2, 0)
-        turn(2, 1)
-        make_shift(1)
+        def store_last(h, t):
+            nc.sync.dma_start(out=y_rows[LAST_GROUP, :, t:t + 2, h * HALF:(h + 1) * HALF], in_=y[LAST_GROUP][:, h, t:t + 2, :])
+
+        def store_scales(q, queue, g0, g1, planes):
+            queue.dma_start(out=out_2[g0:g1, 4 * q:4 * q + 4, :].rearrange("g r m -> r g m").bitcast(I32),
+                            in_=planes[32 * q:32 * q + 4, :, :].bitcast(I32))
+
+        group_b_vector(0)
+        group_b_scalar(0)
+        quantize_b(0)
+        nc.vector.tensor_copy(out=offset[:].rearrange("m (p j) -> m p j", j=PACK), in_=spread[:].rearrange("m j p -> m p j"))
+        for i in range(PACK):
+            turn(i, (0,))
+            quantize_a(i, (0,))
+        group_b_vector(1)
+        group_b_scalar(1)
+        for i in range(PACK):
+            multiply(i, 0)
+        make_shifts(2, 2)
+        quantize_b(1)
+        group_b_vector(2)
+        for i in (0, 1):
+            turn(i, (1,))
+            quantize_a(i, (1,))
+        group_b_scalar(2)
+        for i in range(PACK):
+            multiply(i, 1)
+        quantize_b(2)
+        group_b_vector(3)
+        group_b_scalar(3)
+        quantize_b(3)
+        for i in (2, 3):
+            turn(i, (1,))
+            quantize_a(i, (1,))
+        multiply(0, 2)
+        multiply(1, 2)
+        for i in (4, 5):
+            turn(i)
+            quantize_a(i)
+            make_shifts(i - 1, 1)
         multiply(0, 3)
         multiply(1, 3)
         for i in (2, 3):
             multiply(i, 2)
             multiply(i, 3)
-        quantize_a(2, 1)
         leave_psum(0)
         leave_psum(1)
-        make_shift(2)
-        make_shift(3)
         clamp(0)
         clamp(1)
 
-        last = PAIRS - 1
-        for pair in range(2, last):
-            done = pair - 1
-            g = done // 2
-            leave_psum(2 * done)
-            if done % 2 == 0:
+        for j in range(4, LAST - 2, 2):
+            done = j - 2
+            g = done // PACK
+            closes = done % PACK == 2
+            leave_psum(done)
+            if not closes:
                 quantize_y(g - 1)
-                store_words(g - 1)
-            leave_psum(2 * done + 1)
-            clamp(2 * done)
-            clamp(2 * done + 1)
-            if done % 2 == 1:
-                store_y(g)
-                group_y(nc.vector.tensor_copy, g, 0, HALF)
-            if pair == 2:
-                make_shift(4)
-                make_shift(5)
-            turn(pair + 1, 0)
-            quantize_a(pair + 1, 0)
-            turn(pair + 1, 1)
-            quantize_a(pair + 1, 1)
-            if done % 2 == 1:
-                group_y(nc.scalar.copy, g, HALF, C)
-            make_shift(2 * pair + 2)
-            make_shift(2 * pair + 3)
-            for i in (2 * pair, 2 * pair + 1):
-                for c in range(PASSES):
-                    multiply(i, c)
+                if g - 1 == GROUPS - 3:
+                    for q in range(4):
+                        store_scales(q, nc.sync, 0, GROUPS - 2, y_scales_early)
+            leave_psum(done + 1)
+            clamp(done)
+            clamp(done + 1)
+            compact(j + 4)
+            if closes:
+                nc.sync.dma_start(out=y_rows[g], in_=y[g][:])
+                group_y(nc.vector.tensor_copy, g, 0)
+            compact(j + 5)
+            for i in (j + 2, j + 3):
+                turn(i)
+                quantize_a(i)
+            if j + 2 + 2 * PAIR_BUFS < TILES:
+                load_tiles(j + 2 + 2 * PAIR_BUFS, 2)
+            if j == 4:
+                make_shifts(6, 2)
+            if closes:
+                group_y(nc.scalar.copy, g, 1)
+            make_shifts(j + SHIFT_AHEAD, 2 if closes else 3)
+            all_passes(j)
+            all_passes(j + 1)
 
-        g = GROUPS - 1
-        first, second = 2 * last, 2 * last + 1
+        g = LAST_GROUP
         for lo, tag in ((0, "acc"), (HALF, "turn")):
-            for i in (first, second):
-                for c in range(PASSES):
-                    multiply(i, c, lo, lo + HALF, tag)
-        leave_psum(first - 2)
+            all_passes(LAST - 1, lo, lo + HALF, tag)
+            all_passes(LAST, lo, lo + HALF, tag)
+        leave_psum(LAST - 3)
         quantize_y(g - 1)
-        store_words(g - 1)
-        for q in range(4):
-            nc.sync.dma_start(out=out_2[0:g, 4 * q:4 * q + 4, :].rearrange("g r m -> r g m").bitcast(I32),
-                              in_=y_scales[32 * q:32 * q + 4, :, :].bitcast(I32))
-        leave_psum(first - 1)
-        clamp(first - 2)
-        leave_psum(first, 0, HALF)
-        clamp(first - 1)
-        store_y(g, 0, 2)
-        leave_psum(second, 0, HALF)
-        clamp(first, 0, HALF)
-        clamp(second, 0, HALF)
-        store_y(g, 2, 4, 0, HALF)
-        group_y(nc.scalar.copy, g, 0, HALF)
-        leave_psum(first, HALF, C)
-        leave_psum(second, HALF, C)
-        clamp(first, HALF, C)
-        clamp(second, HALF, C)
-        store_y(g, 2, 4, HALF, C)
-        group_y(nc.vector.tensor_copy, g, HALF, C)
+        leave_psum(LAST - 2)
+        clamp(LAST - 3)
+        leave_psum(LAST - 1, 0, HALF)
+        clamp(LAST - 2)
+        store_last(0, 0)
+        store_last(1, 0)
+        leave_psum(LAST, 0, HALF)
+        clamp(LAST - 1, 0, HALF)
+        leave_psum(LAST - 1, HALF, C)
+        clamp(LAST, 0, HALF)
+        store_last(0, 2)
+        group_y(nc.scalar.copy, g, 0)
+        leave_psum(LAST, HALF, C)
+        clamp(LAST - 1, HALF, C)
+        clamp(LAST, HALF, C)
+        store_last(1, 2)
+        group_y(nc.vector.tensor_copy, g, 1)
         quantize_y(g, 0, HALF)
-        store_words(g, 0, HALF)
         quantize_y(g, HALF, C)
-        store_words(g, HALF, C)
         for q in range(4):
-            queue = nc.scalar if q < 2 else nc.sync
-            queue.dma_start(out=out_2[g, 4 * q:4 * q + 4, :].bitcast(I32),
-                            in_=y_scales_last[32 * q:32 * q + 4, :].bitcast(I32))
+            store_scales(q, nc.scalar if q < 2 else nc.sync, g - 1, GROUPS, y_scales_late)

@@ -99,9 +99,6 @@ def tile_clamped_two_hop_labels_g2_kernel(tc, two_hop, labels, class_offset, nod
         weight = keep.tile([P, GROUPS, PACK], F32, name="weight")
         upper = keep.tile([P, GROUPS, PACK], F32, name="upper")
         lower = keep.tile([P, GROUPS, PACK], F32, name="lower")
-        nc.vector.tensor_copy(out=weight[:], in_=weight_raw[:, :, 0:PACK])
-        nc.vector.scalar_tensor_tensor(out=upper[:], in0=weight[:], scalar=-1.0, in1=weight[:], op0=ALU.mult, op1=ALU.max)
-        nc.vector.scalar_tensor_tensor(out=lower[:], in0=weight[:], scalar=-1.0, in1=weight[:], op0=ALU.mult, op1=ALU.min)
 
         y_scales_early = keep.tile([P, GROUPS - 2, C], U8, name="y_scales_early", align_bytes=64)
         y_scales_late = keep.tile([P, 2, C], U8, name="y_scales_late", align_bytes=64)
@@ -139,7 +136,7 @@ def tile_clamped_two_hop_labels_g2_kernel(tc, two_hop, labels, class_offset, nod
                                   in_=a_grouped[i][:])
 
         def interleave(copy, dst, src):
-            copy(out=dst.rearrange("p (c i) t -> p c t i", i=4), in_=src.rearrange("p t (c i) -> p c t i", i=4))
+            copy(out=dst, in_=src.rearrange("p t c -> p c t"))
 
         def group_b_vector(c):
             grouped = work.tile([P, C, PACK], BF16, tag="b_grouped", name="b_grouped_tile", align_bytes=64)
@@ -232,6 +229,11 @@ def tile_clamped_two_hop_labels_g2_kernel(tc, two_hop, labels, class_offset, nod
         for i in range(PACK):
             turn(i, (0,))
             quantize_a(i, (0,))
+            if i == 1:
+                nc.vector.tensor_copy(out=weight[:], in_=weight_raw[:, :, 0:PACK])
+            if i == 2:
+                nc.vector.scalar_tensor_tensor(out=upper[:], in0=weight[:], scalar=-1.0, in1=weight[:], op0=ALU.mult, op1=ALU.max)
+                nc.vector.scalar_tensor_tensor(out=lower[:], in0=weight[:], scalar=-1.0, in1=weight[:], op0=ALU.mult, op1=ALU.min)
         group_b_vector(1)
         group_b_scalar(1)
         for i in range(PACK):

@@ -25,11 +25,10 @@ K_HALF = K // 2
 HALF = C // 2
 LAST_GROUP = GROUPS - 1
 LAST = TILES - 1
-B_VECTOR_COLS = 320
+B_VECTOR_COLS = 352
 SINGLE_TILES = 6
-PAIR_BUFS = 6
-COMPACT_FROM, COMPACT_TO = 10, 22
 SHIFT_AHEAD = 6
+YV = (384, 384, 384, 384, 0)
 
 
 def tile_clamped_two_hop_labels_g2_kernel(tc, two_hop, labels, class_offset, node_weight,
@@ -53,7 +52,7 @@ def tile_clamped_two_hop_labels_g2_kernel(tc, two_hop, labels, class_offset, nod
         nc.scalar.dma_start(out=weight_raw[:, :, 0:PACK],
                             in_=node_weight.rearrange("(g p t) -> p g t", p=P, t=PACK))
 
-        a_words, a_odd, a_grouped, a_codes, a_scales = {}, {}, {}, {}, {}
+        a_words, a_grouped, a_codes, a_scales = {}, {}, {}, {}
         b_raw, b_grouped, b_codes, b_scales = {}, {}, {}, {}
         acc, shift, y, y_grouped, y_codes = {}, {}, {}, {}, {}
 
@@ -64,7 +63,7 @@ def tile_clamped_two_hop_labels_g2_kernel(tc, two_hop, labels, class_offset, nod
 
         def load_tiles(first, count):
             g, t = first // PACK, first % PACK
-            raw = work.tile([P, count, K], BF16, tag="a_raw_%d" % count, name="raw", bufs=PAIR_BUFS if count == 2 else 2)
+            raw = keep.tile([P, count, K], BF16, name="a_raw_%d" % first)
             nc.sync.dma_start(out=raw[:], in_=a_rows[g, :, t:t + count, :])
             for n in range(count):
                 a_words[first + n] = raw[:, n, :].bitcast(F32)
@@ -87,7 +86,7 @@ def tile_clamped_two_hop_labels_g2_kernel(tc, two_hop, labels, class_offset, nod
             load_labels(c)
         for i in range(PACK, SINGLE_TILES):
             load_tiles(i, 1)
-        for i in range(SINGLE_TILES, SINGLE_TILES + 2 * PAIR_BUFS, 2):
+        for i in range(SINGLE_TILES, TILES, 2):
             load_tiles(i, 2)
 
         offset_col = keep.tile([P, PACK], F32, name="offset_col")
@@ -103,20 +102,12 @@ def tile_clamped_two_hop_labels_g2_kernel(tc, two_hop, labels, class_offset, nod
         y_scales_early = keep.tile([P, GROUPS - 2, C], U8, name="y_scales_early", align_bytes=64)
         y_scales_late = keep.tile([P, 2, C], U8, name="y_scales_late", align_bytes=64)
 
-        def compact(i):
-            if COMPACT_FROM <= i < COMPACT_TO:
-                odd = work.tile([P, PASSES * P], F32, tag="a_odd", name="odd", bufs=4)
-                nc.vector.tensor_copy(out=odd[:], in_=a_words[i][:, 1::2])
-                a_odd[i] = odd
-
         def turn_half(i, kh, grouped):
             bank = psum.tile([P, 2, 2, P], F32, tag="turn", name="bank")
             for cl in range(2):
                 words = a_words[i, kh][:, 2 * P * cl:2 * P * (cl + 1)]
-                c = 2 * kh + cl
-                nc.tensor.transpose(bank[:, cl, 0, :], words[:, 0::2], ident[:])
-                nc.tensor.transpose(bank[:, cl, 1, :],
-                                    a_odd[i][:, c * P:(c + 1) * P] if i in a_odd else words[:, 1::2], ident[:])
+                for u in range(2):
+                    nc.tensor.transpose(bank[:, cl, u, :], words[:, u::2], ident[:])
             nc.scalar.copy(out=grouped.bitcast(F32).rearrange("p (c r u) -> p c r u", c=2, u=2),
                            in_=bank[:].rearrange("p c u r -> p c r u"))
 
@@ -136,7 +127,7 @@ def tile_clamped_two_hop_labels_g2_kernel(tc, two_hop, labels, class_offset, nod
                                   in_=a_grouped[i][:])
 
         def interleave(copy, dst, src):
-            copy(out=dst, in_=src.rearrange("p t c -> p c t"))
+            copy(out=dst.rearrange("p (c i) t -> p c t i", i=4), in_=src.rearrange("p t (c i) -> p c t i", i=4))
 
         def group_b_vector(c):
             grouped = work.tile([P, C, PACK], BF16, tag="b_grouped", name="b_grouped_tile", align_bytes=64)
@@ -167,11 +158,14 @@ def tile_clamped_two_hop_labels_g2_kernel(tc, two_hop, labels, class_offset, nod
             for c in range(PASSES):
                 multiply(i, c, lo, hi, tag)
 
-        def make_shifts(upto, most):
+        def make_shifts(upto, most, vector=False):
             for i in range(len(shift), min(len(shift) + most, upto, TILES)):
-                tile_shift = work.tile([P, C], F32, tag="shift", name="tile_shift", bufs=8)
-                nc.scalar.activation(out=tile_shift[:], in_=offset[:], func=ACT.Copy,
-                                     scale=weight[:, i // PACK, i % PACK:i % PACK + 1])
+                tile_shift = work.tile([P, C], F32, tag="shift", name="tile_shift", bufs=7)
+                factor = weight[:, i // PACK, i % PACK:i % PACK + 1]
+                if vector:
+                    nc.vector.tensor_scalar(out=tile_shift[:], in0=offset[:], scalar1=factor, scalar2=None, op0=ALU.mult)
+                else:
+                    nc.scalar.activation(out=tile_shift[:], in_=offset[:], func=ACT.Copy, scale=factor)
                 shift[i] = tile_shift
 
         def y_part(i, lo, hi):
@@ -180,8 +174,8 @@ def tile_clamped_two_hop_labels_g2_kernel(tc, two_hop, labels, class_offset, nod
                 return y[g][:, lo // HALF:hi // HALF, t, :]
             return y[g][:, t, lo:hi].rearrange("p (h c) -> p h c", c=HALF)
 
-        def y_half(g, h):
-            return y[g][:, h, :, :] if g == LAST_GROUP else y[g][:, :, h * HALF:(h + 1) * HALF]
+        def y_cols(g, lo, hi):
+            return y[g][:, lo // HALF, :, lo % HALF:lo % HALF + hi - lo] if g == LAST_GROUP else y[g][:, :, lo:hi]
 
         def leave_psum(i, lo=0, hi=C):
             g, t = i // PACK, i % PACK
@@ -199,11 +193,13 @@ def tile_clamped_two_hop_labels_g2_kernel(tc, two_hop, labels, class_offset, nod
             nc.vector.tensor_scalar(out=y_part(i, lo, hi), in0=y_part(i, lo, hi), scalar1=lower[:, g, t:t + 1],
                                     scalar2=upper[:, g, t:t + 1], op0=ALU.max, op1=ALU.min)
 
-        def group_y(copy, g, h):
+        def group_y(copy, g, lo, hi):
+            if lo == hi:
+                return
             if g not in y_grouped:
                 grouped = work.tile([P, C, PACK], BF16, tag="y_grouped", name="y_grouped_tile", align_bytes=64)
                 y_grouped[g] = grouped
-            interleave(copy, y_grouped[g][:, h * HALF:(h + 1) * HALF, :], y_half(g, h))
+            interleave(copy, y_grouped[g][:, lo:hi, :], y_cols(g, lo, hi))
 
         def quantize_y(g, lo=0, hi=C):
             if g not in y_codes:
@@ -238,33 +234,35 @@ def tile_clamped_two_hop_labels_g2_kernel(tc, two_hop, labels, class_offset, nod
         group_b_scalar(1)
         for i in range(PACK):
             multiply(i, 0)
-        make_shifts(2, 2)
+        make_shifts(1, 1)
         quantize_b(1)
         group_b_vector(2)
+        group_b_scalar(2)
         for i in (0, 1):
             turn(i, (1,))
             quantize_a(i, (1,))
-        group_b_scalar(2)
         for i in range(PACK):
             multiply(i, 1)
         quantize_b(2)
         group_b_vector(3)
         group_b_scalar(3)
-        quantize_b(3)
         for i in (2, 3):
             turn(i, (1,))
             quantize_a(i, (1,))
+        quantize_b(3)
         multiply(0, 2)
         multiply(1, 2)
-        for i in (4, 5):
-            turn(i)
-            quantize_a(i)
-            make_shifts(i - 1, 1)
+        make_shifts(2, 2, True)
+        turn(4)
+        quantize_a(4)
+        turn(5)
+        make_shifts(4, 2)
         multiply(0, 3)
         multiply(1, 3)
         for i in (2, 3):
             multiply(i, 2)
             multiply(i, 3)
+        quantize_a(5)
         leave_psum(0)
         leave_psum(1)
         clamp(0)
@@ -283,20 +281,16 @@ def tile_clamped_two_hop_labels_g2_kernel(tc, two_hop, labels, class_offset, nod
             leave_psum(done + 1)
             clamp(done)
             clamp(done + 1)
-            compact(j + 4)
             if closes:
                 nc.sync.dma_start(out=y_rows[g], in_=y[g][:])
-                group_y(nc.vector.tensor_copy, g, 0)
-            compact(j + 5)
+                group_y(nc.vector.tensor_copy, g, 0, YV[g])
             for i in (j + 2, j + 3):
                 turn(i)
                 quantize_a(i)
-            if j + 2 + 2 * PAIR_BUFS < TILES:
-                load_tiles(j + 2 + 2 * PAIR_BUFS, 2)
             if j == 4:
                 make_shifts(6, 2)
             if closes:
-                group_y(nc.scalar.copy, g, 1)
+                group_y(nc.scalar.copy, g, YV[g], C)
             make_shifts(j + SHIFT_AHEAD, 2 if closes else 3)
             all_passes(j)
             all_passes(j + 1)
@@ -306,7 +300,6 @@ def tile_clamped_two_hop_labels_g2_kernel(tc, two_hop, labels, class_offset, nod
             all_passes(LAST - 1, lo, lo + HALF, tag)
             all_passes(LAST, lo, lo + HALF, tag)
         leave_psum(LAST - 3)
-        quantize_y(g - 1)
         leave_psum(LAST - 2)
         clamp(LAST - 3)
         leave_psum(LAST - 1, 0, HALF)
@@ -318,12 +311,14 @@ def tile_clamped_two_hop_labels_g2_kernel(tc, two_hop, labels, class_offset, nod
         leave_psum(LAST - 1, HALF, C)
         clamp(LAST, 0, HALF)
         store_last(0, 2)
-        group_y(nc.scalar.copy, g, 0)
+        group_y(nc.scalar.copy, g, 0, HALF)
         leave_psum(LAST, HALF, C)
         clamp(LAST - 1, HALF, C)
         clamp(LAST, HALF, C)
         store_last(1, 2)
-        group_y(nc.vector.tensor_copy, g, 1)
+        quantize_y(g - 1)
+        group_y(nc.scalar.copy, g, C - 64, C)
+        group_y(nc.vector.tensor_copy, g, HALF, C - 64)
         quantize_y(g, 0, HALF)
         quantize_y(g, HALF, C)
         for q in range(4):

from contextlib import ExitStack

import concourse.mybir as mybir
from concourse.masks import make_identity

T, K, C = 3072, 2048, 512
FLOPS = 2 * T * K * C

F32 = mybir.dt.float32
BF16 = mybir.dt.bfloat16
U32 = mybir.dt.uint32
I32 = mybir.dt.int32
U8 = mybir.dt.uint8
FP8X4 = mybir.dt.float8_e4m3fn_x4
ALU = mybir.AluOpType
ACT = mybir.ActivationFunctionType

P = 128
PACK = 4
K_PASS = P * PACK
PASSES = K // K_PASS
GROUPS = T // K_PASS
TILES = T // P
K_HALF = K // 2
HALF = C // 2
LAST_GROUP = GROUPS - 1
LAST = TILES - 1
B_VECTOR_COLS = 352
SINGLE_TILES = 6
SHIFT_AHEAD = 6
YV = (384, 384, 384, 384, 0)


def tile_clamped_two_hop_labels_g2_kernel(tc, two_hop, labels, class_offset, node_weight,
                                                     out_0, out_1, out_2):
    nc = tc.nc
    a_rows = two_hop.rearrange("(g p t) k -> g p t k", p=P, t=PACK)
    y_rows = out_0.rearrange("(g p t) c -> g p t c", p=P, t=PACK)

    with ExitStack() as ctx:
        keep = ctx.enter_context(tc.tile_pool(name="keep", bufs=1))
        work = ctx.enter_context(tc.tile_pool(name="work", bufs=2))
        psum = ctx.enter_context(tc.psum_pool(name="psum", bufs=4))
        ctx.enter_context(tc.manual_schedule())

        ident = keep.tile([P, P], F32, name="ident")
        make_identity(nc, ident[:])

        offset_raw = keep.tile([P, PACK], BF16, name="offset_raw")
        nc.scalar.dma_start(out=offset_raw[:], in_=class_offset.rearrange("(p j) -> p j", j=PACK))
        weight_raw = keep.tile([P, GROUPS, 16], BF16, name="weight_raw")
        nc.scalar.dma_start(out=weight_raw[:, :, 0:PACK],
                            in_=node_weight.rearrange("(g p t) -> p g t", p=P, t=PACK))

        a_words, a_grouped, a_codes, a_scales = {}, {}, {}, {}
        b_raw, b_grouped, b_codes, b_scales = {}, {}, {}, {}
        acc, shift, y, y_grouped, y_codes = {}, {}, {}, {}, {}

        def load_half(i, kh):
            raw = keep.tile([P, K_HALF], BF16, name="a_half_%d_%d" % (i, kh))
            nc.sync.dma_start(out=raw[:], in_=a_rows[0, :, i, kh * K_HALF:(kh + 1) * K_HALF])
            a_words[i, kh] = raw[:].bitcast(F32)

        def load_tiles(first, count):
            g, t = first // PACK, first % PACK
            raw = keep.tile([P, count, K], BF16, name="a_raw_%d" % first)
            nc.sync.dma_start(out=raw[:], in_=a_rows[g, :, t:t + count, :])
            for n in range(count):
                a_words[first + n] = raw[:, n, :].bitcast(F32)
                for kh in range(2):
                    a_words[first + n, kh] = a_words[first + n][:, kh * K_HALF // 2:(kh + 1) * K_HALF // 2]

        def load_labels(c):
            raw = keep.tile([P, PACK, C], BF16, name="b_raw_%d" % c)
            nc.sync.dma_start(out=raw[:],
                              in_=labels[c * K_PASS:(c + 1) * K_PASS, :].rearrange("(p j) n -> p j n", j=PACK))
            b_raw[c] = raw

        load_labels(0)
        for i in range(PACK):
            load_half(i, 0)
        load_labels(1)
        for c in (2, 3):
            load_half(2 * c - 4, 1)
            load_half(2 * c - 3, 1)
            load_labels(c)
        for i in range(PACK, SINGLE_TILES):
            load_tiles(i, 1)
        for i in range(SINGLE_TILES, TILES, 2):
            load_tiles(i, 2)

        offset_col = keep.tile([P, PACK], F32, name="offset_col")
        nc.vector.tensor_copy(out=offset_col[:], in_=offset_raw[:])
        spread = psum.tile([P, PACK, P], F32, tag="turn", name="spread")
        for j in range(PACK):
            nc.tensor.transpose(spread[:, j, :], offset_col[:, j:j + 1].to_broadcast([P, P]), ident[:])
        offset = keep.tile([P, C], F32, name="offset")
        weight = keep.tile([P, GROUPS, PACK], F32, name="weight")
        upper = keep.tile([P, GROUPS, PACK], F32, name="upper")
        lower = keep.tile([P, GROUPS, PACK], F32, name="lower")

        y_scales_early = keep.tile([P, GROUPS - 2, C], U8, name="y_scales_early", align_bytes=64)
        y_scales_late = keep.tile([P, 2, C], U8, name="y_scales_late", align_bytes=64)

        def turn_half(i, kh, grouped):
            bank = psum.tile([P, 2, 2, P], F32, tag="turn", name="bank")
            for cl in range(2):
                words = a_words[i, kh][:, 2 * P * cl:2 * P * (cl + 1)]
                for u in range(2):
                    nc.tensor.transpose(bank[:, cl, u, :], words[:, u::2], ident[:])
            nc.scalar.copy(out=grouped.bitcast(F32).rearrange("p (c r u) -> p c r u", c=2, u=2),
                           in_=bank[:].rearrange("p c u r -> p c r u"))

        def turn(i, halves=(0, 1)):
            grouped = work.tile([P, len(halves) * K_HALF], BF16, tag="a_grouped", name="grouped", bufs=4, align_bytes=64)
            for n, kh in enumerate(halves):
                turn_half(i, kh, grouped[:, n * K_HALF:(n + 1) * K_HALF])
            a_grouped[i] = grouped

        def quantize_a(i, halves=(0, 1)):
            if halves[0] == 0:
                codes = work.tile([P, PASSES * P], U32, tag="a_codes", name="codes", bufs=6, align_bytes=64)
                scales = work.tile([P, PASSES * P], U8, tag="a_scales", name="scales", bufs=6, align_bytes=64)
                a_codes[i], a_scales[i] = codes, scales
            cols = slice(2 * P * halves[0], 2 * P * (halves[-1] + 1))
            nc.vector.quantize_mx(out=a_codes[i][:, cols].bitcast(FP8X4), scales=a_scales[i][:, cols],
                                  in_=a_grouped[i][:])

        def interleave(copy, dst, src):
            copy(out=dst.rearrange("p (c i) t -> p c t i", i=4), in_=src.rearrange("p t (c i) -> p c t i", i=4))

        def group_b_vector(c):
            grouped = work.tile([P, C, PACK], BF16, tag="b_grouped", name="b_grouped_tile", align_bytes=64)
            interleave(nc.vector.tensor_copy, grouped[:, :B_VECTOR_COLS, :], b_raw[c][:, :, :B_VECTOR_COLS])
            b_grouped[c] = grouped

        def group_b_scalar(c):
            interleave(nc.scalar.copy, b_grouped[c][:, B_VECTOR_COLS:, :], b_raw[c][:, :, B_VECTOR_COLS:])

        def quantize_b(c):
            codes = keep.tile([P, C], U32, name="b_codes_%d" % c, align_bytes=64)
            scales = keep.tile([P, C], U8, name="b_scales_%d" % c, align_bytes=64)
            nc.vector.quantize_mx(out=codes[:].bitcast(FP8X4), scales=scales[:],
                                  in_=b_grouped[c][:].rearrange("p n j -> p (n j)"))
            b_codes[c], b_scales[c] = codes, scales

        def multiply(i, c, lo=0, hi=C, tag="acc"):
            if c == 0:
                bank = psum.tile([P, hi - lo], F32, tag=tag, name="acc_bank")
                acc[i, lo] = bank
            cols = slice(c * P, (c + 1) * P)
            nc.tensor.matmul_mx(out=acc[i, lo][:],
                                lhsT=a_codes[i][:, cols].bitcast(FP8X4), lhsT_scale=a_scales[i][:, cols],
                                rhs=b_codes[c][:, lo:hi].bitcast(FP8X4), rhs_scale=b_scales[c][:, lo:hi],
                                start=(c == 0), stop=(c == PASSES - 1))

        def all_passes(i, lo=0, hi=C, tag="acc"):
            for c in range(PASSES):
                multiply(i, c, lo, hi, tag)

        def make_shifts(upto, most, vector=False):
            for i in range(len(shift), min(len(shift) + most, upto, TILES)):
                tile_shift = work.tile([P, C], F32, tag="shift", name="tile_shift", bufs=7)
                factor = weight[:, i // PACK, i % PACK:i % PACK + 1]
                if vector:
                    nc.vector.tensor_scalar(out=tile_shift[:], in0=offset[:], scalar1=factor, scalar2=None, op0=ALU.mult)
                else:
                    nc.scalar.activation(out=tile_shift[:], in_=offset[:], func=ACT.Copy, scale=factor)
                shift[i] = tile_shift

        def y_part(i, lo, hi):
            g, t = i // PACK, i % PACK
            if g == LAST_GROUP:
                return y[g][:, lo // HALF:hi // HALF, t, :]
            return y[g][:, t, lo:hi].rearrange("p (h c) -> p h c", c=HALF)

        def y_cols(g, lo, hi):
            return y[g][:, lo // HALF, :, lo % HALF:lo % HALF + hi - lo] if g == LAST_GROUP else y[g][:, :, lo:hi]

        def leave_psum(i, lo=0, hi=C):
            g, t = i // PACK, i % PACK
            if g not in y:
                y_group = work.tile([P, 2, PACK, HALF] if g == LAST_GROUP else [P, PACK, C], F32, tag="y",
                                    name="y_group", bufs=4)
                y[g] = y_group
            nc.vector.scalar_tensor_tensor(out=y_part(i, lo, hi), in0=acc[i, lo][:].rearrange("p (h c) -> p h c", c=HALF),
                                           scalar=weight[:, g, t:t + 1],
                                           in1=shift[i][:, lo:hi].rearrange("p (h c) -> p h c", c=HALF),
                                           op0=ALU.mult, op1=ALU.add)

        def clamp(i, lo=0, hi=C):
            g, t = i // PACK, i % PACK
            nc.vector.tensor_scalar(out=y_part(i, lo, hi), in0=y_part(i, lo, hi), scalar1=lower[:, g, t:t + 1],
                                    scalar2=upper[:, g, t:t + 1], op0=ALU.max, op1=ALU.min)

        def group_y(copy, g, lo, hi):
            if lo == hi:
                return
            if g not in y_grouped:
                grouped = work.tile([P, C, PACK], BF16, tag="y_grouped", name="y_grouped_tile", align_bytes=64)
                y_grouped[g] = grouped
            interleave(copy, y_grouped[g][:, lo:hi, :], y_cols(g, lo, hi))

        def quantize_y(g, lo=0, hi=C):
            if g not in y_codes:
                codes = keep.tile([P, C], U32, name="y_codes_%d" % g, align_bytes=64)
                y_codes[g] = codes
            scales = y_scales_early[:, g, lo:hi] if g < GROUPS - 2 else y_scales_late[:, g - (GROUPS - 2), lo:hi]
            nc.vector.quantize_mx(out=y_codes[g][:, lo:hi].bitcast(FP8X4), scales=scales,
                                  in_=y_grouped[g][:, lo:hi, :].rearrange("p n j -> p (n j)"))
            nc.sync.dma_start(out=out_1[g, :, lo:hi, :].rearrange("p m t -> p (m t)").bitcast(I32),
                              in_=y_codes[g][:, lo:hi].bitcast(I32))

        def store_last(h, t):
            nc.sync.dma_start(out=y_rows[LAST_GROUP, :, t:t + 2, h * HALF:(h + 1) * HALF], in_=y[LAST_GROUP][:, h, t:t + 2, :])

        def store_scales(q, queue, g0, g1, planes):
            queue.dma_start(out=out_2[g0:g1, 4 * q:4 * q + 4, :].rearrange("g r m -> r g m").bitcast(I32),
                            in_=planes[32 * q:32 * q + 4, :, :].bitcast(I32))

        group_b_vector(0)
        group_b_scalar(0)
        quantize_b(0)
        nc.vector.tensor_copy(out=offset[:].rearrange("m (p j) -> m p j", j=PACK), in_=spread[:].rearrange("m j p -> m p j"))
        for i in range(PACK):
            turn(i, (0,))
            quantize_a(i, (0,))
            if i == 1:
                nc.vector.tensor_copy(out=weight[:], in_=weight_raw[:, :, 0:PACK])
            if i == 2:
                nc.vector.scalar_tensor_tensor(out=upper[:], in0=weight[:], scalar=-1.0, in1=weight[:], op0=ALU.mult, op1=ALU.max)
                nc.vector.scalar_tensor_tensor(out=lower[:], in0=weight[:], scalar=-1.0, in1=weight[:], op0=ALU.mult, op1=ALU.min)
        group_b_vector(1)
        group_b_scalar(1)
        for i in range(PACK):
            multiply(i, 0)
        make_shifts(1, 1)
        quantize_b(1)
        group_b_vector(2)
        group_b_scalar(2)
        for i in (0, 1):
            turn(i, (1,))
            quantize_a(i, (1,))
        for i in range(PACK):
            multiply(i, 1)
        quantize_b(2)
        group_b_vector(3)
        group_b_scalar(3)
        for i in (2, 3):
            turn(i, (1,))
            quantize_a(i, (1,))
        quantize_b(3)
        multiply(0, 2)
        multiply(1, 2)
        make_shifts(2, 2, True)
        turn(4)
        quantize_a(4)
        turn(5)
        make_shifts(4, 2)
        multiply(0, 3)
        multiply(1, 3)
        for i in (2, 3):
            multiply(i, 2)
            multiply(i, 3)
        quantize_a(5)
        leave_psum(0)
        leave_psum(1)
        clamp(0)
        clamp(1)

        for j in range(4, LAST - 2, 2):
            done = j - 2
            g = done // PACK
            closes = done % PACK == 2
            leave_psum(done)
            if not closes:
                quantize_y(g - 1)
                if g - 1 == GROUPS - 3:
                    for q in range(4):
                        store_scales(q, nc.sync, 0, GROUPS - 2, y_scales_early)
            leave_psum(done + 1)
            clamp(done)
            clamp(done + 1)
            if closes:
                nc.sync.dma_start(out=y_rows[g], in_=y[g][:])
                group_y(nc.vector.tensor_copy, g, 0, YV[g])
            for i in (j + 2, j + 3):
                turn(i)
                quantize_a(i)
            if j == 4:
                make_shifts(6, 2)
            if closes:
                group_y(nc.scalar.copy, g, YV[g], C)
            make_shifts(j + SHIFT_AHEAD, 2 if closes else 3)
            all_passes(j)
            all_passes(j + 1)

        g = LAST_GROUP
        for lo, tag in ((0, "acc"), (HALF, "turn")):
            all_passes(LAST - 1, lo, lo + HALF, tag)
            all_passes(LAST, lo, lo + HALF, tag)
        leave_psum(LAST - 3)
        leave_psum(LAST - 2)
        clamp(LAST - 3)
        leave_psum(LAST - 1, 0, HALF)
        clamp(LAST - 2)
        store_last(0, 0)
        store_last(1, 0)
        leave_psum(LAST, 0, HALF)
        clamp(LAST - 1, 0, HALF)
        leave_psum(LAST - 1, HALF, C)
        clamp(LAST, 0, HALF)
        store_last(0, 2)
        group_y(nc.scalar.copy, g, 0, HALF)
        leave_psum(LAST, HALF, C)
        clamp(LAST - 1, HALF, C)
        clamp(LAST, HALF, C)
        store_last(1, 2)
        quantize_y(g - 1)
        group_y(nc.scalar.copy, g, C - 64, C)
        group_y(nc.vector.tensor_copy, g, HALF, C - 64)
        quantize_y(g, 0, HALF)
        quantize_y(g, HALF, C)
        for q in range(4):
            store_scales(q, nc.scalar if q < 2 else nc.sync, g - 1, GROUPS, y_scales_late)
